import numpy as np
CORES = [20,21,28,29]
N = 4
ROOT = 3
def setup_inputs(rng):
    return {"x": rng.standard_normal((N, 128, 1024), dtype=np.float32)}
def reference(x):
    y = np.full((N, 128, N * 1024), np.nan, x.dtype)
    y[ROOT] = np.concatenate(list(x), axis=1)
    return {"y": y}

PIECE = 512
NPIECES = 6
HELPER = {0: 22, 1: 18, 2: 23, 3: 19}

SCRATCH = {
    "buf": ("sbuf", [128, NPIECES * PIECE], "float32"),
}
SEMAPHORES = ["ld0", "ld1", "hop", "sent", "stored"] + ["a%d" % p for p in range(NPIECES)]


def _engines(mask):
    return bin(mask).count("1")


def _send(g, T, topo, src, dst, piece, remote_sem):
    rid, pid, _se = topo.addr(dst)
    m = topo.mask(src, dst)
    cols = T.buf[:, piece * PIECE:(piece + 1) * PIECE]
    g.remote_dma(cols, cols, remote_sem, T.sem.sent, pid, rid, m)
    return _engines(m)


def rank_program(g, core, T, topo):
    rank = T.rank_of(core)
    root = T.cores[T.root]

    if rank is None:
        for piece, helper in HELPER.items():
            if helper == core:
                sender = T.cores[piece // 2]
                g.wait_ge(T.sem.hop, _engines(topo.mask(sender, core)))
                n = _send(g, T, topo, core, root, piece, T.sem["a%d" % piece])
                g.wait_ge(T.sem.sent, n)
        return

    if core == root:
        g.sync.dma_start(T.y[:, NPIECES * PIECE:], T.x[:]).then_inc(T.sem.stored, 16)
        for queue, pieces in ((g.sync, (4, 0, 2)), (g.scalar, (5, 1, 3))):
            for piece in pieces:
                last = HELPER.get(piece, T.cores[piece // 2])
                queue.wait_ge(T.sem["a%d" % piece], _engines(topo.mask(last, core)))
                cols = slice(piece * PIECE, (piece + 1) * PIECE)
                queue.dma_start(T.y[:, cols], T.buf[:, cols]).then_inc(T.sem.stored, 16)
        g.wait_ge(T.sem.stored, 16 * (NPIECES + 1))
        return

    for half, queue in ((0, g.sync), (1, g.scalar)):
        piece = 2 * rank + half
        queue.dma_start(T.buf[:, piece * PIECE:(piece + 1) * PIECE],
                        T.x[:, half * PIECE:(half + 1) * PIECE]).then_inc(T.sem["ld%d" % half], 16)
    left = 0
    for half in (0, 1):
        piece = 2 * rank + half
        g.wait_ge(T.sem["ld%d" % half], 16)
        if topo.may_write(core, root):
            left += _send(g, T, topo, core, root, piece, T.sem["a%d" % piece])
        else:
            left += _send(g, T, topo, core, HELPER[piece], piece, T.sem.hop)
    g.wait_ge(T.sem.sent, left)
